import numpy as np
import ml_dtypes


def mxq(x, axis, fmt="e4m3"):
    dtype, down = {"e4m3": (ml_dtypes.float8_e4m3fn, 7), "e5m2": (ml_dtypes.float8_e5m2, 14)}[fmt]
    v = np.moveaxis(np.asarray(x, np.float32).astype(ml_dtypes.bfloat16).astype(np.float64), axis, -1)
    blocks = v.reshape(v.shape[:-1] + (-1, 32))
    amax = np.abs(blocks).max(-1, keepdims=True)
    byte = np.maximum(np.where(amax > 0, np.frexp(amax)[1] - 1 + 127, 0) - down, 1)
    scale = np.exp2(byte - 127.0)
    codes = (blocks / scale).astype(np.float32).astype(dtype).astype(np.float64)
    return np.moveaxis((codes * scale).reshape(v.shape), -1, axis)


WIDE = False


def mx_kscale(k):
    if not WIDE:
        return np.ones(k)
    levels = np.array([10, -10, 5, -5, 0])
    if k % 512:
        return np.exp2(np.random.permutation(np.resize(levels, k // 32))).repeat(32)
    a = np.empty((k // 512, 16))
    for p in range(k // 512):
        a[p, :8] = np.random.permutation(np.resize(levels, 8))
        for g in range(8):
            far = levels[np.abs(levels - a[p, g]) >= 10]
            a[p, g + 8] = far[np.random.randint(len(far))]
    return np.exp2(a.ravel()).repeat(32)


def f64(x):
    return np.asarray(x).astype(np.float64)


def striped(idx):
    return np.tile(np.asarray(idx).reshape(-1, 16).T, (8, 1)).astype(np.uint16)


def unstriped(offs):
    return offs[:16].T.reshape(-1).astype(np.int64)


E2M1 = np.array([0.0, 0.5, 1.0, 1.5, 2.0, 3.0, 4.0, 6.0, -0.0, -0.5, -1.0, -1.5, -2.0, -3.0, -4.0, -6.0])


def pack_weight(w, fmt):
    k, n = w.shape
    w = f64(np.asarray(w, np.float32).astype(ml_dtypes.bfloat16)).reshape(k // 32, 32, n)
    amax = np.abs(w).max(1)
    if fmt == "e4m3":
        byte = np.frexp(amax)[1] - 1 + 127 - 7
    else:
        mant, ex = np.frexp(amax / 6.0)
        byte = np.where(mant > 0.5, ex, ex - 1) + 127
    byte = np.clip(np.where(amax > 0, byte, 1), 1, 254)
    scaled = (w * np.exp2(127.0 - byte)[:, None, :]).reshape(k, n).astype(np.float32)
    by_word = np.ascontiguousarray(scaled.reshape(k // 512, 128, 4, n).transpose(0, 1, 3, 2))
    if fmt == "e4m3":
        words = by_word.astype(ml_dtypes.float8_e4m3fn).view(np.uint8)
    else:
        c = by_word.astype(ml_dtypes.float4_e2m1fn).view(np.uint8) & 0xF
        words = (c[..., 0::2] | (c[..., 1::2] << 4)).reshape(k // 512, 128, 2 * n)
    return np.ascontiguousarray(words), np.ascontiguousarray(byte.astype(np.uint8).reshape(k // 512, 16, n))


def unpack_weight(words, scales, fmt):
    g, _, n = scales.shape
    words = np.ascontiguousarray(words).reshape(g, 128, n, -1)
    if fmt == "e4m3":
        vals = words.view(ml_dtypes.float8_e4m3fn).astype(np.float64)
    else:
        nib = np.empty((g, 128, n, 4), np.uint8)
        nib[..., 0::2] = words & 0xF
        nib[..., 1::2] = words >> 4
        vals = E2M1[nib]
    vals = vals * np.repeat(np.exp2(scales.astype(np.float64) - 127.0), 8, axis=1)[..., None]
    return vals.transpose(0, 1, 3, 2).reshape(g * 512, n)


def bf(x):
    return np.asarray(x, np.float32).astype(ml_dtypes.bfloat16)


def planes(Y):
    r, m = Y.shape
    b = f64(bf(Y)).reshape(r // 32, 32, m)
    amax = np.abs(b).max(1)
    byte = np.clip(np.where(amax > 0, np.frexp(amax)[1] - 1 + 127 - 7, 1), 1, 254)
    codes = (b * np.exp2(127.0 - byte)[:, None, :]).reshape(r, m).astype(np.float32).astype(ml_dtypes.float8_e4m3fn).view(np.uint8)
    words = codes.reshape(r // 512, 128, 4, m).transpose(0, 1, 3, 2)
    return np.ascontiguousarray(words), np.ascontiguousarray(byte.astype(np.uint8).reshape(r // 512, 16, m))


K, J, T, N = 2048, 512, 512, 512


def setup_inputs():
    n = np.random.standard_normal
    idx = np.random.permutation(K)[:J]
    fk = mx_kscale(K)
    fj = mx_kscale(J)
    tj = np.ones(K)
    tj[idx] = fj
    xo = n((T, K))
    xo[:, idx] *= 6.0
    xr = xo.copy()
    xr[:, idx] = 0.0
    xbp = pack_weight(xr.T / fk[:, None], "e2m1")
    wbp = pack_weight(n((K, N)) * 1 / np.sqrt(K) * fk[:, None], "e4m3")
    wop = pack_weight(n((J, N)) * 1 / np.sqrt(J) * fj[:, None], "e2m1")
    return {
        "xb_words": xbp[0],
        "xb_scales": xbp[1],
        "wb_words": wbp[0],
        "wb_scales": wbp[1],
        "xt": (xo / tj).astype(np.float32),
        "wo_words": wop[0],
        "wo_scales": wop[1],
        "offs": striped(idx),
    }


def reference(xb_words, xb_scales, wb_words, wb_scales, xt, wo_words, wo_scales, offs):
    idx = unstriped(offs)
    xbu = unpack_weight(xb_words, xb_scales, "e2m1")
    wbu = unpack_weight(wb_words, wb_scales, "e4m3")
    wou = unpack_weight(wo_words, wo_scales, "e2m1")
    xo = f64(xt)[:, idx].T
    xoq = mxq(xo, 0, "e4m3")
    y = wbu.T @ xbu + wou.T @ xoq
    words, scales = planes(y)
    return y, words, scales

@@ -1,0 +1,182 @@
+from contextlib import ExitStack
+
+import concourse.mybir as mybir
+from concourse.masks import make_identity
+
+K, J, T, N = 2048, 512, 512, 512
+FLOPS = 2 * (K + J) * T * N
+
+F32 = mybir.dt.float32
+BF16 = mybir.dt.bfloat16
+I32 = mybir.dt.int32
+U32 = mybir.dt.uint32
+U16 = mybir.dt.uint16
+U8 = mybir.dt.uint8
+E4M3X4 = mybir.dt.float8_e4m3fn_x4
+E2M1X4 = mybir.dt.float4_e2m1fn_x4
+
+P = 128
+PACK = 4
+PASSES = K // (P * PACK)
+TILES = T // P
+QUADS = 4
+
+
+def load_scale_rows(queue, plane, rows):
+    passes = rows.shape[0]
+    for q in range(QUADS):
+        queue.dma_start(
+            out=plane[32 * q : 32 * q + 4, :].bitcast(I32).rearrange("r (z c) -> r z c", z=passes),
+            in_=rows[:, 4 * q : 4 * q + 4, :].bitcast(I32).rearrange("z r c -> r z c"),
+        )
+
+
+def tile_list_outlier_channels_pl_kernel(
+    tc, xb_words, xb_scales, wb_words, wb_scales, xt, wo_words, wo_scales, offs, out_0, out_1, out_2
+):
+    nc = tc.nc
+    y_rows = out_0.rearrange("(p r) t -> p r t", r=PACK)
+    code_rows = out_1[0].rearrange("p c r -> p (c r)").bitcast(I32)
+
+    with ExitStack() as ctx:
+        keep = ctx.enter_context(tc.tile_pool(name="keep", bufs=1))
+        acc_pool = ctx.enter_context(tc.psum_pool(name="acc", bufs=1))
+        turn_pool = ctx.enter_context(tc.psum_pool(name="turn", bufs=2))
+
+        offsets = keep.tile([P, J // 16], U16, name="offsets")
+        wb_scale_raw = keep.tile([P, PASSES * N], U8, name="wb_scale_raw", align_bytes=64)
+        xb_scale = keep.tile([P, PASSES * T], U8, name="xb_scale", align_bytes=64)
+        wo_scale_raw = keep.tile([P, N], U8, name="wo_scale_raw", align_bytes=64)
+        ident = keep.tile([P, P], F32, name="ident")
+        wb_raw = [keep.tile([P, 2, N], U32, name="wb_raw%d" % h) for h in range(2)]
+        xb = keep.tile([P, PASSES, 2 * T], U8, name="xb", align_bytes=64)
+        wo_raw = keep.tile([P, 2 * N], U8, name="wo_raw", align_bytes=64)
+        rows = [keep.tile([P, K], F32, name="rows%d" % i) for i in range(TILES)]
+
+        def load_wb(h):
+            nc.sync.dma_start(
+                out=wb_raw[h][:].bitcast(I32),
+                in_=wb_words[2 * h : 2 * h + 2].rearrange("z p n r -> p z (n r)").bitcast(I32),
+            )
+
+        def load_rows(i):
+            nc.sync.dma_start(out=rows[i][:], in_=xt[P * i : P * (i + 1), :])
+
+        nc.gpsimd.memset(wb_scale_raw[:].bitcast(U32), 0)
+        nc.vector.memset(xb_scale[:].bitcast(U32), 0)
+        nc.vector.memset(wo_scale_raw[:].bitcast(U32), 0)
+        make_identity(nc, ident[:])
+        load_wb(0)
+        nc.sync.dma_start(out=xb[:].bitcast(I32), in_=xb_words.rearrange("z p c -> p z c").bitcast(I32))
+        load_scale_rows(nc.scalar, wb_scale_raw, wb_scales)
+        load_scale_rows(nc.scalar, xb_scale, xb_scales)
+        load_wb(1)
+        load_rows(0)
+        nc.sync.dma_start(offsets[:], offs)
+        load_scale_rows(nc.scalar, wo_scale_raw, wo_scales)
+        load_rows(1)
+        nc.sync.dma_start(out=wo_raw[:].bitcast(I32), in_=wo_words[0].bitcast(I32))
+        load_rows(2)
+        load_rows(3)
+
+        wb_scale = [keep.tile([P, N], U8, name="wb_scale%d" % z, align_bytes=64) for z in range(PASSES)]
+        wb = [keep.tile([P, N], U32, name="wb%d" % z, align_bytes=64) for z in range(PASSES)]
+        wo_scale = keep.tile([P, N], U8, name="wo_scale", align_bytes=64)
+        wo = keep.tile([P, N], U16, name="wo", align_bytes=64)
+
+        def deal(dealt, raw):
+            nc.vector.tensor_copy(
+                out=dealt.rearrange("p (r m) -> p r m", r=PACK), in_=raw.rearrange("p (m r) -> p r m", r=PACK)
+            )
+
+        for z in range(PASSES):
+            deal(wb_scale[z][:], wb_scale_raw[:, N * z : N * (z + 1)])
+            deal(wb[z][:], wb_raw[z // 2][:, z % 2, :])
+
+        acc = [acc_pool.tile([P, PACK, P], F32, name="acc%d" % i) for i in range(TILES)]
+        grouped = [keep.tile([P, P * PACK], BF16, name="grouped%d" % i, align_bytes=64) for i in range(TILES + 1)]
+        xo = [keep.tile([P, P], U32, name="xo%d" % i, align_bytes=64) for i in range(TILES)]
+        xo_scale = [keep.tile([P, P], U8, name="xo_scale%d" % i, align_bytes=64) for i in range(TILES)]
+        y = keep.tile([P, PACK, T], F32, name="y")
+        y_codes = keep.tile([P, T], U32, name="y_codes", align_bytes=64)
+        y_scale = keep.tile([P, T], U8, name="y_scale", align_bytes=64)
+
+        def base(i):
+            for z in range(PASSES):
+                for r in range(PACK):
+                    nc.tensor.matmul_mx(
+                        out=acc[i][:, r, :],
+                        lhsT=wb[z][:, P * r : P * (r + 1)].bitcast(E4M3X4),
+                        lhsT_scale=wb_scale[z][:, P * r : P * (r + 1)],
+                        rhs=xb[:, z, 2 * P * i : 2 * P * (i + 1)].bitcast(E2M1X4),
+                        rhs_scale=xb_scale[:, T * z + P * i : T * z + P * (i + 1)],
+                        start=(z == 0 and r == 0),
+                        stop=False,
+                    )
+
+        def pick(i):
+            picked = keep.tile([P, J], BF16, name="picked%d" % i)
+            nc.vector.tensor_copy(picked[:], rows[i][:].indirect(offsets[:]))
+            pairs = picked[:].bitcast(F32)
+            turned = turn_pool.tile([P, 2, P], F32, name="turned")
+            for u in range(2):
+                nc.tensor.transpose(turned[:, u, :], pairs[:, u : J // 2 : 2], ident[:])
+            nc.scalar.copy(
+                out=grouped[i][:].bitcast(F32).rearrange("p (t u) -> p t u", u=2),
+                in_=turned[:].rearrange("p u t -> p t u"),
+            )
+            nc.vector.quantize_mx(out=xo[i][:].bitcast(E4M3X4), scales=xo_scale[i][:], in_=grouped[i][:])
+
+        def finish(i):
+            for r in range(PACK):
+                nc.tensor.matmul_mx(
+                    out=acc[i][:, r, :],
+                    lhsT=wo[:, P * r : P * (r + 1)].bitcast(E2M1X4),
+                    lhsT_scale=wo_scale[:, P * r : P * (r + 1)],
+                    rhs=xo[i][:].bitcast(E4M3X4),
+                    rhs_scale=xo_scale[i][:],
+                    start=False,
+                    stop=(r == PACK - 1),
+                )
+            nc.scalar.copy(out=y[:, :, P * i : P * (i + 1)], in_=acc[i][:])
+            if i > 0:
+                stored = slice(0 if i == 1 else P * i, P * (i + 1))
+                nc.sync.dma_start(out=y_rows[:, :, stored], in_=y[:, :, stored])
+
+        def planes(i):
+            tokens = slice(P * i, P * (i + 1))
+            nc.vector.tensor_copy(
+                out=grouped[i + 1][:].rearrange("p (t r) -> p t r", r=PACK),
+                in_=y[:, :, tokens].rearrange("p r t -> p t r"),
+            )
+            nc.vector.quantize_mx(
+                out=y_codes[:, tokens].bitcast(E4M3X4), scales=y_scale[:, tokens], in_=grouped[i + 1][:]
+            )
+            if i >= TILES - 2:
+                stored = slice(0 if i == TILES - 2 else P * i, P * (i + 1))
+                nc.sync.dma_start(out=code_rows[:, stored], in_=y_codes[:, stored].bitcast(I32))
+
+        base(0)
+        pick(0)
+        base(1)
+        deal(wo[:], wo_raw[:].bitcast(U16))
+        deal(wo_scale[:], wo_scale_raw[:])
+        finish(0)
+        pick(1)
+        base(2)
+        planes(0)
+        finish(1)
+        base(3)
+        pick(2)
+        planes(1)
+        finish(2)
+        pick(3)
+        planes(2)
+        finish(3)
+        planes(3)
+
+        for q in range(QUADS):
+            nc.scalar.dma_start(
+                out=out_2[0, 4 * q : 4 * q + 4, :].bitcast(I32),
+                in_=y_scale[32 * q : 32 * q + 4, :].bitcast(I32),
+            )

@@ -48,16 +48,10 @@ def tile_list_outlier_channels_pl_kernel(
         xb_scale = keep.tile([P, PASSES * T], U8, name="xb_scale", align_bytes=64)
         wo_scale_raw = keep.tile([P, N], U8, name="wo_scale_raw", align_bytes=64)
         ident = keep.tile([P, P], F32, name="ident")
-        wb_raw = [keep.tile([P, 2, N], U32, name="wb_raw%d" % h) for h in range(2)]
+        wb_raw = keep.tile([P, PASSES, N], U32, name="wb_raw")
         xb = keep.tile([P, PASSES, 2 * T], U8, name="xb", align_bytes=64)
         wo_raw = keep.tile([P, 2 * N], U8, name="wo_raw", align_bytes=64)
-        rows = [keep.tile([P, K], F32, name="rows%d" % i) for i in range(TILES)]
-
-        def load_wb(h):
-            nc.sync.dma_start(
-                out=wb_raw[h][:].bitcast(I32),
-                in_=wb_words[2 * h : 2 * h + 2].rearrange("z p n r -> p z (n r)").bitcast(I32),
-            )
+        rows = [keep.tile([P, K], F32, name="rows%d" % i, tag="rows%d" % i, align_bytes=64) for i in range(TILES)]
 
         def load_rows(i):
             nc.sync.dma_start(out=rows[i][:], in_=xt[P * i : P * (i + 1), :])
@@ -66,16 +60,17 @@ def tile_list_outlier_channels_pl_kernel(
         nc.vector.memset(xb_scale[:].bitcast(U32), 0)
         nc.vector.memset(wo_scale_raw[:].bitcast(U32), 0)
         make_identity(nc, ident[:])
-        load_wb(0)
+        warm = keep.tile([P, 1], F32, name="warm")
+        nc.scalar.copy(out=warm[:], in_=ident[:, 0:1])
         nc.sync.dma_start(out=xb[:].bitcast(I32), in_=xb_words.rearrange("z p c -> p z c").bitcast(I32))
-        load_scale_rows(nc.scalar, wb_scale_raw, wb_scales)
-        load_scale_rows(nc.scalar, xb_scale, xb_scales)
-        load_wb(1)
+        load_scale_rows(nc.sync, wb_scale_raw, wb_scales)
+        nc.sync.dma_start(out=wb_raw[:].bitcast(I32), in_=wb_words.rearrange("z p n r -> p z (n r)").bitcast(I32))
+        load_scale_rows(nc.sync, xb_scale, xb_scales)
         load_rows(0)
         nc.sync.dma_start(offsets[:], offs)
-        load_scale_rows(nc.scalar, wo_scale_raw, wo_scales)
         load_rows(1)
         nc.sync.dma_start(out=wo_raw[:].bitcast(I32), in_=wo_words[0].bitcast(I32))
+        load_scale_rows(nc.sync, wo_scale_raw, wo_scales)
         load_rows(2)
         load_rows(3)
 
@@ -84,48 +79,52 @@ def tile_list_outlier_channels_pl_kernel(
         wo_scale = keep.tile([P, N], U8, name="wo_scale", align_bytes=64)
         wo = keep.tile([P, N], U16, name="wo", align_bytes=64)
 
-        def deal(dealt, raw):
+        def deal(dealt, raw, run):
             nc.vector.tensor_copy(
-                out=dealt.rearrange("p (r m) -> p r m", r=PACK), in_=raw.rearrange("p (m r) -> p r m", r=PACK)
+                out=dealt.rearrange("p (r c i) -> p c r i", r=PACK, i=run),
+                in_=raw.rearrange("p (c i r) -> p c r i", r=PACK, i=run),
             )
 
         for z in range(PASSES):
-            deal(wb_scale[z][:], wb_scale_raw[:, N * z : N * (z + 1)])
-            deal(wb[z][:], wb_raw[z // 2][:, z % 2, :])
+            deal(wb_scale[z][:], wb_scale_raw[:, N * z : N * (z + 1)], 16)
+        for z in range(PASSES):
+            deal(wb[z][:], wb_raw[:, z, :], 4)
 
         acc = [acc_pool.tile([P, PACK, P], F32, name="acc%d" % i) for i in range(TILES)]
-        grouped = [keep.tile([P, P * PACK], BF16, name="grouped%d" % i, align_bytes=64) for i in range(TILES + 1)]
+        turned = [turn_pool.tile([P, 2, P], F32, name="turned%d" % i, tag="turned") for i in range(TILES)]
         xo = [keep.tile([P, P], U32, name="xo%d" % i, align_bytes=64) for i in range(TILES)]
         xo_scale = [keep.tile([P, P], U8, name="xo_scale%d" % i, align_bytes=64) for i in range(TILES)]
         y = keep.tile([P, PACK, T], F32, name="y")
         y_codes = keep.tile([P, T], U32, name="y_codes", align_bytes=64)
         y_scale = keep.tile([P, T], U8, name="y_scale", align_bytes=64)
 
-        def base(i):
-            for z in range(PASSES):
-                for r in range(PACK):
-                    nc.tensor.matmul_mx(
-                        out=acc[i][:, r, :],
-                        lhsT=wb[z][:, P * r : P * (r + 1)].bitcast(E4M3X4),
-                        lhsT_scale=wb_scale[z][:, P * r : P * (r + 1)],
-                        rhs=xb[:, z, 2 * P * i : 2 * P * (i + 1)].bitcast(E2M1X4),
-                        rhs_scale=xb_scale[:, T * z + P * i : T * z + P * (i + 1)],
-                        start=(z == 0 and r == 0),
-                        stop=False,
-                    )
+        def base():
+            for i in range(TILES):
+                for z in range(PASSES):
+                    for r in range(PACK):
+                        nc.tensor.matmul_mx(
+                            out=acc[i][:, r, :],
+                            lhsT=wb[z][:, P * r : P * (r + 1)].bitcast(E4M3X4),
+                            lhsT_scale=wb_scale[z][:, P * r : P * (r + 1)],
+                            rhs=xb[:, z, 2 * P * i : 2 * P * (i + 1)].bitcast(E2M1X4),
+                            rhs_scale=xb_scale[:, T * z + P * i : T * z + P * (i + 1)],
+                            start=(z == 0 and r == 0),
+                            stop=False,
+                        )
 
-        def pick(i):
+        def gather(i):
             picked = keep.tile([P, J], BF16, name="picked%d" % i)
             nc.vector.tensor_copy(picked[:], rows[i][:].indirect(offsets[:]))
             pairs = picked[:].bitcast(F32)
-            turned = turn_pool.tile([P, 2, P], F32, name="turned")
             for u in range(2):
-                nc.tensor.transpose(turned[:, u, :], pairs[:, u : J // 2 : 2], ident[:])
+                nc.tensor.transpose(turned[i][:, u, :], pairs[:, u : J // 2 : 2], ident[:])
+
+        def quantise(i, grouped):
             nc.scalar.copy(
-                out=grouped[i][:].bitcast(F32).rearrange("p (t u) -> p t u", u=2),
-                in_=turned[:].rearrange("p u t -> p t u"),
+                out=grouped.bitcast(F32).rearrange("p (t u) -> p t u", u=2),
+                in_=turned[i][:].rearrange("p u t -> p t u"),
             )
-            nc.vector.quantize_mx(out=xo[i][:].bitcast(E4M3X4), scales=xo_scale[i][:], in_=grouped[i][:])
+            nc.vector.quantize_mx(out=xo[i][:].bitcast(E4M3X4), scales=xo_scale[i][:], in_=grouped)
 
         def finish(i):
             for r in range(PACK):
@@ -143,37 +142,36 @@ def tile_list_outlier_channels_pl_kernel(
                 stored = slice(0 if i == 1 else P * i, P * (i + 1))
                 nc.sync.dma_start(out=y_rows[:, :, stored], in_=y[:, :, stored])
 
-        def planes(i):
+        def planes(i, grouped):
             tokens = slice(P * i, P * (i + 1))
             nc.vector.tensor_copy(
-                out=grouped[i + 1][:].rearrange("p (t r) -> p t r", r=PACK),
-                in_=y[:, :, tokens].rearrange("p r t -> p t r"),
+                out=grouped.rearrange("p (c i r) -> p c r i", r=PACK, i=4),
+                in_=y[:, :, tokens].rearrange("p r (c i) -> p c r i", i=4),
             )
             nc.vector.quantize_mx(
-                out=y_codes[:, tokens].bitcast(E4M3X4), scales=y_scale[:, tokens], in_=grouped[i + 1][:]
+                out=y_codes[:, tokens].bitcast(E4M3X4), scales=y_scale[:, tokens], in_=grouped
             )
             if i >= TILES - 2:
                 stored = slice(0 if i == TILES - 2 else P * i, P * (i + 1))
                 nc.sync.dma_start(out=code_rows[:, stored], in_=y_codes[:, stored].bitcast(I32))
 
-        base(0)
-        pick(0)
-        base(1)
-        deal(wo[:], wo_raw[:].bitcast(U16))
-        deal(wo_scale[:], wo_scale_raw[:])
-        finish(0)
-        pick(1)
-        base(2)
-        planes(0)
-        finish(1)
-        base(3)
-        pick(2)
-        planes(1)
-        finish(2)
-        pick(3)
-        planes(2)
-        finish(3)
-        planes(3)
+        gather(0)
+        base()
+        for i in range(1, TILES):
+            gather(i)
+            if i == 1:
+                deal(wo[:], wo_raw[:].bitcast(U16), 8)
+                deal(wo_scale[:], wo_scale_raw[:], 16)
+            spare = keep.tile([P, 2, P * PACK], BF16, name="spare%d" % i, tag="rows%d" % i, align_bytes=64)
+            quantise(i - 1, spare[:, 0, :])
+            if i >= 2:
+                planes(i - 2, spare[:, 1, :])
+            finish(i - 1)
+        last = keep.tile([P, 2, P * PACK], BF16, name="last", align_bytes=64)
+        quantise(TILES - 1, last[:, 0, :])
+        planes(TILES - 2, last[:, 0, :])
+        finish(TILES - 1)
+        planes(TILES - 1, last[:, 1, :])
 
         for q in range(QUADS):
             nc.scalar.dma_start(

@@ -24,10 +24,10 @@ QUADS = 4
 
 def load_scale_rows(queue, plane, rows):
     passes = rows.shape[0]
-    for q in range(QUADS):
+    for r in range(4):
         queue.dma_start(
-            out=plane[32 * q : 32 * q + 4, :].bitcast(I32).rearrange("r (z c) -> r z c", z=passes),
-            in_=rows[:, 4 * q : 4 * q + 4, :].bitcast(I32).rearrange("z r c -> r z c"),
+            out=plane[r:P:32, :].bitcast(I32).rearrange("q (z c) -> q z c", z=passes),
+            in_=rows[:, r:16:4, :].bitcast(I32).rearrange("z q c -> q z c"),
         )
 
 
@@ -46,7 +46,7 @@ def tile_list_outlier_channels_pl_kernel(
         offsets = keep.tile([P, J // 16], U16, name="offsets")
         wb_scale_raw = keep.tile([P, PASSES * N], U8, name="wb_scale_raw", align_bytes=64)
         xb_scale = keep.tile([P, PASSES * T], U8, name="xb_scale", align_bytes=64)
-        wo_scale_raw = keep.tile([P, N], U8, name="wo_scale_raw", align_bytes=64)
+        wo_scale_raw = keep.tile([P, N], U8, name="wo_scale_raw", tag="wo_scale_raw", align_bytes=64)
         ident = keep.tile([P, P], F32, name="ident")
         wb_raw = keep.tile([P, PASSES, N], U32, name="wb_raw")
         xb = keep.tile([P, PASSES, 2 * T], U8, name="xb", align_bytes=64)
@@ -90,7 +90,7 @@ def tile_list_outlier_channels_pl_kernel(
         for z in range(PASSES):
             deal(wb[z][:], wb_raw[:, z, :], 4)
 
-        acc = [acc_pool.tile([P, PACK, P], F32, name="acc%d" % i) for i in range(TILES)]
+        acc = []
         turned = [turn_pool.tile([P, 2, P], F32, name="turned%d" % i, tag="turned") for i in range(TILES)]
         xo = [keep.tile([P, P], U32, name="xo%d" % i, align_bytes=64) for i in range(TILES)]
         xo_scale = [keep.tile([P, P], U8, name="xo_scale%d" % i, align_bytes=64) for i in range(TILES)]
@@ -98,19 +98,19 @@ def tile_list_outlier_channels_pl_kernel(
         y_codes = keep.tile([P, T], U32, name="y_codes", align_bytes=64)
         y_scale = keep.tile([P, T], U8, name="y_scale", align_bytes=64)
 
-        def base():
-            for i in range(TILES):
-                for z in range(PASSES):
-                    for r in range(PACK):
-                        nc.tensor.matmul_mx(
-                            out=acc[i][:, r, :],
-                            lhsT=wb[z][:, P * r : P * (r + 1)].bitcast(E4M3X4),
-                            lhsT_scale=wb_scale[z][:, P * r : P * (r + 1)],
-                            rhs=xb[:, z, 2 * P * i : 2 * P * (i + 1)].bitcast(E2M1X4),
-                            rhs_scale=xb_scale[:, T * z + P * i : T * z + P * (i + 1)],
-                            start=(z == 0 and r == 0),
-                            stop=False,
-                        )
+        def base(i):
+            acc.append(acc_pool.tile([P, PACK, P], F32, name="acc%d" % i, tag="acc%d" % (i % 3)))
+            for z in range(PASSES):
+                for r in range(PACK):
+                    nc.tensor.matmul_mx(
+                        out=acc[i][:, r, :],
+                        lhsT=wb[z][:, P * r : P * (r + 1)].bitcast(E4M3X4),
+                        lhsT_scale=wb_scale[z][:, P * r : P * (r + 1)],
+                        rhs=xb[:, z, 2 * P * i : 2 * P * (i + 1)].bitcast(E2M1X4),
+                        rhs_scale=xb_scale[:, T * z + P * i : T * z + P * (i + 1)],
+                        start=(z == 0 and r == 0),
+                        stop=False,
+                    )
 
         def gather(i):
             picked = keep.tile([P, J], BF16, name="picked%d" % i)
@@ -142,39 +142,44 @@ def tile_list_outlier_channels_pl_kernel(
                 stored = slice(0 if i == 1 else P * i, P * (i + 1))
                 nc.sync.dma_start(out=y_rows[:, :, stored], in_=y[:, :, stored])
 
-        def planes(i, grouped):
-            tokens = slice(P * i, P * (i + 1))
+        def planes(tokens, grouped):
             nc.vector.tensor_copy(
                 out=grouped.rearrange("p (c i r) -> p c r i", r=PACK, i=4),
                 in_=y[:, :, tokens].rearrange("p r (c i) -> p c r i", i=4),
             )
-            nc.vector.quantize_mx(
-                out=y_codes[:, tokens].bitcast(E4M3X4), scales=y_scale[:, tokens], in_=grouped
-            )
-            if i >= TILES - 2:
-                stored = slice(0 if i == TILES - 2 else P * i, P * (i + 1))
-                nc.sync.dma_start(out=code_rows[:, stored], in_=y_codes[:, stored].bitcast(I32))
+            nc.vector.quantize_mx(out=y_codes[:, tokens].bitcast(E4M3X4), scales=y_scale[:, tokens], in_=grouped)
+
+        def store_codes(tokens):
+            nc.sync.dma_start(out=code_rows[:, tokens], in_=y_codes[:, tokens].bitcast(I32))
+
+        def staging(name, tiles, tag):
+            return keep.tile([P, tiles * P * PACK], BF16, name=name, tag=tag, align_bytes=64)[:]
 
         gather(0)
-        base()
-        for i in range(1, TILES):
-            gather(i)
-            if i == 1:
-                deal(wo[:], wo_raw[:].bitcast(U16), 8)
-                deal(wo_scale[:], wo_scale_raw[:], 16)
-            spare = keep.tile([P, 2, P * PACK], BF16, name="spare%d" % i, tag="rows%d" % i, align_bytes=64)
-            quantise(i - 1, spare[:, 0, :])
-            if i >= 2:
-                planes(i - 2, spare[:, 1, :])
-            finish(i - 1)
-        last = keep.tile([P, 2, P * PACK], BF16, name="last", align_bytes=64)
-        quantise(TILES - 1, last[:, 0, :])
-        planes(TILES - 2, last[:, 0, :])
-        finish(TILES - 1)
-        planes(TILES - 1, last[:, 1, :])
+        for i in range(3):
+            base(i)
+        gather(1)
+        deal(wo[:], wo_raw[:].bitcast(U16), 8)
+        deal(wo_scale[:], wo_scale_raw[:], 16)
+        first_in = staging("first_in", 2, "wo_scale_raw")
+        quantise(0, first_in[:, 0:T])
+        quantise(1, first_in[:, T : 2 * T])
+        finish(0)
+        finish(1)
+        gather(2)
+        base(3)
+        gather(3)
+        after_3 = staging("after_3", 3, "rows3")
+        planes(slice(0, 2 * P), after_3[:, 0 : 2 * T])
+        quantise(2, after_3[:, 2 * T : 3 * T])
+        finish(2)
+        last_in = staging("last_in", 1, "last_in")
+        quantise(3, last_in)
+        planes(slice(2 * P, 3 * P), last_in)
+        store_codes(slice(0, 3 * P))
+        finish(3)
+        planes(slice(3 * P, T), staging("y_in3", 1, "y_in3"))
+        store_codes(slice(3 * P, T))
 
-        for q in range(QUADS):
-            nc.scalar.dma_start(
-                out=out_2[0, 4 * q : 4 * q + 4, :].bitcast(I32),
-                in_=y_scale[32 * q : 32 * q + 4, :].bitcast(I32),
-            )
+        for r in range(4):
+            nc.scalar.dma_start(out=out_2[0, r:16:4, :].bitcast(I32), in_=y_scale[r:P:32, :].bitcast(I32))

@@ -19,15 +19,19 @@ P = 128
 PACK = 4
 PASSES = K // (P * PACK)
 TILES = T // P
-QUADS = 4
+BLOCKS = 16
+QUADRANT = 32
+SCALE_ROWS = 4
+LINE = 16
+WIDE = P * PACK
+BANKS = TILES - 1
 
 
-def load_scale_rows(queue, plane, rows):
-    passes = rows.shape[0]
-    for r in range(4):
-        queue.dma_start(
-            out=plane[r:P:32, :].bitcast(I32).rearrange("q (z c) -> q z c", z=passes),
-            in_=rows[:, r:16:4, :].bitcast(I32).rearrange("z q c -> q z c"),
+def load_scale_rows(nc, plane, rows):
+    for s in range(SCALE_ROWS):
+        nc.sync.dma_start(
+            out=plane[s:P:QUADRANT, :].bitcast(I32).rearrange("q (z c) -> q z c", z=rows.shape[0]),
+            in_=rows[:, s:BLOCKS:SCALE_ROWS, :].bitcast(I32).rearrange("z q c -> q z c"),
         )
 
 
@@ -59,18 +63,19 @@ def tile_list_outlier_channels_pl_kernel(
         nc.gpsimd.memset(wb_scale_raw[:].bitcast(U32), 0)
         nc.vector.memset(xb_scale[:].bitcast(U32), 0)
         nc.vector.memset(wo_scale_raw[:].bitcast(U32), 0)
-        make_identity(nc, ident[:])
-        warm = keep.tile([P, 1], F32, name="warm")
-        nc.scalar.copy(out=warm[:], in_=ident[:, 0:1])
+        ident_bf16 = keep.tile([P, P], BF16, name="ident_bf16")
+        make_identity(nc, ident_bf16[:])
+        nc.scalar.copy(out=ident[:], in_=ident_bf16[:])
+
         nc.sync.dma_start(out=xb[:].bitcast(I32), in_=xb_words.rearrange("z p c -> p z c").bitcast(I32))
-        load_scale_rows(nc.sync, wb_scale_raw, wb_scales)
+        load_scale_rows(nc, wb_scale_raw, wb_scales)
         nc.sync.dma_start(out=wb_raw[:].bitcast(I32), in_=wb_words.rearrange("z p n r -> p z (n r)").bitcast(I32))
-        load_scale_rows(nc.sync, xb_scale, xb_scales)
+        load_scale_rows(nc, xb_scale, xb_scales)
         load_rows(0)
         nc.sync.dma_start(offsets[:], offs)
         load_rows(1)
         nc.sync.dma_start(out=wo_raw[:].bitcast(I32), in_=wo_words[0].bitcast(I32))
-        load_scale_rows(nc.sync, wo_scale_raw, wo_scales)
+        load_scale_rows(nc, wo_scale_raw, wo_scales)
         load_rows(2)
         load_rows(3)
 
@@ -79,14 +84,15 @@ def tile_list_outlier_channels_pl_kernel(
         wo_scale = keep.tile([P, N], U8, name="wo_scale", align_bytes=64)
         wo = keep.tile([P, N], U16, name="wo", align_bytes=64)
 
-        def deal(dealt, raw, run):
+        def deal(dealt, raw, item_bytes):
+            run = LINE // item_bytes
             nc.vector.tensor_copy(
                 out=dealt.rearrange("p (r c i) -> p c r i", r=PACK, i=run),
                 in_=raw.rearrange("p (c i r) -> p c r i", r=PACK, i=run),
             )
 
         for z in range(PASSES):
-            deal(wb_scale[z][:], wb_scale_raw[:, N * z : N * (z + 1)], 16)
+            deal(wb_scale[z][:], wb_scale_raw[:, N * z : N * (z + 1)], 1)
         for z in range(PASSES):
             deal(wb[z][:], wb_raw[:, z, :], 4)
 
@@ -98,8 +104,11 @@ def tile_list_outlier_channels_pl_kernel(
         y_codes = keep.tile([P, T], U32, name="y_codes", align_bytes=64)
         y_scale = keep.tile([P, T], U8, name="y_scale", align_bytes=64)
 
+        def tokens(first, count):
+            return slice(P * first, P * (first + count))
+
         def base(i):
-            acc.append(acc_pool.tile([P, PACK, P], F32, name="acc%d" % i, tag="acc%d" % (i % 3)))
+            acc.append(acc_pool.tile([P, PACK, P], F32, name="acc%d" % i, tag="acc%d" % (i % BANKS)))
             for z in range(PASSES):
                 for r in range(PACK):
                     nc.tensor.matmul_mx(
@@ -119,12 +128,12 @@ def tile_list_outlier_channels_pl_kernel(
             for u in range(2):
                 nc.tensor.transpose(turned[i][:, u, :], pairs[:, u : J // 2 : 2], ident[:])
 
-        def quantise(i, grouped):
+        def quantise_xo(i, staged):
             nc.scalar.copy(
-                out=grouped.bitcast(F32).rearrange("p (t u) -> p t u", u=2),
+                out=staged.bitcast(F32).rearrange("p (t u) -> p t u", u=2),
                 in_=turned[i][:].rearrange("p u t -> p t u"),
             )
-            nc.vector.quantize_mx(out=xo[i][:].bitcast(E4M3X4), scales=xo_scale[i][:], in_=grouped)
+            nc.vector.quantize_mx(out=xo[i][:].bitcast(E4M3X4), scales=xo_scale[i][:], in_=staged)
 
         def finish(i):
             for r in range(PACK):
@@ -137,49 +146,56 @@ def tile_list_outlier_channels_pl_kernel(
                     start=False,
                     stop=(r == PACK - 1),
                 )
-            nc.scalar.copy(out=y[:, :, P * i : P * (i + 1)], in_=acc[i][:])
-            if i > 0:
-                stored = slice(0 if i == 1 else P * i, P * (i + 1))
-                nc.sync.dma_start(out=y_rows[:, :, stored], in_=y[:, :, stored])
+            nc.scalar.copy(out=y[:, :, tokens(i, 1)], in_=acc[i][:])
 
-        def planes(tokens, grouped):
+        def quantise_y(cols, staged):
+            run = LINE // 4
             nc.vector.tensor_copy(
-                out=grouped.rearrange("p (c i r) -> p c r i", r=PACK, i=4),
-                in_=y[:, :, tokens].rearrange("p r (c i) -> p c r i", i=4),
+                out=staged.rearrange("p (c i r) -> p c r i", r=PACK, i=run),
+                in_=y[:, :, cols].rearrange("p r (c i) -> p c r i", i=run),
             )
-            nc.vector.quantize_mx(out=y_codes[:, tokens].bitcast(E4M3X4), scales=y_scale[:, tokens], in_=grouped)
+            nc.vector.quantize_mx(out=y_codes[:, cols].bitcast(E4M3X4), scales=y_scale[:, cols], in_=staged)
 
-        def store_codes(tokens):
-            nc.sync.dma_start(out=code_rows[:, tokens], in_=y_codes[:, tokens].bitcast(I32))
+        def store_y(cols):
+            nc.sync.dma_start(out=y_rows[:, :, cols], in_=y[:, :, cols])
+
+        def store_codes(queue, cols):
+            queue.dma_start(out=code_rows[:, cols], in_=y_codes[:, cols].bitcast(I32))
 
         def staging(name, tiles, tag):
-            return keep.tile([P, tiles * P * PACK], BF16, name=name, tag=tag, align_bytes=64)[:]
+            return keep.tile([P, tiles * WIDE], BF16, name=name, tag=tag, align_bytes=64)[:]
 
         gather(0)
-        for i in range(3):
+        for i in range(BANKS):
             base(i)
         gather(1)
-        deal(wo[:], wo_raw[:].bitcast(U16), 8)
-        deal(wo_scale[:], wo_scale_raw[:], 16)
+        deal(wo[:], wo_raw[:].bitcast(U16), 2)
+        deal(wo_scale[:], wo_scale_raw[:], 1)
         first_in = staging("first_in", 2, "wo_scale_raw")
-        quantise(0, first_in[:, 0:T])
-        quantise(1, first_in[:, T : 2 * T])
+        quantise_xo(0, first_in[:, 0:WIDE])
+        quantise_xo(1, first_in[:, WIDE : 2 * WIDE])
         finish(0)
         finish(1)
+        store_y(tokens(0, 2))
         gather(2)
         base(3)
         gather(3)
-        after_3 = staging("after_3", 3, "rows3")
-        planes(slice(0, 2 * P), after_3[:, 0 : 2 * T])
-        quantise(2, after_3[:, 2 * T : 3 * T])
+        after_last = staging("after_last", 3, "rows3")
+        quantise_y(tokens(0, 2), after_last[:, 0 : 2 * WIDE])
+        store_codes(nc.sync, tokens(0, 2))
+        quantise_xo(2, after_last[:, 2 * WIDE : 3 * WIDE])
         finish(2)
+        store_y(tokens(2, 1))
         last_in = staging("last_in", 1, "last_in")
-        quantise(3, last_in)
-        planes(slice(2 * P, 3 * P), last_in)
-        store_codes(slice(0, 3 * P))
+        quantise_xo(3, last_in)
+        quantise_y(tokens(2, 1), last_in)
         finish(3)
-        planes(slice(3 * P, T), staging("y_in3", 1, "y_in3"))
-        store_codes(slice(3 * P, T))
+        store_y(tokens(3, 1))
+        quantise_y(tokens(3, 1), staging("y_in3", 1, "y_in3"))
 
-        for r in range(4):
-            nc.scalar.dma_start(out=out_2[0, r:16:4, :].bitcast(I32), in_=y_scale[r:P:32, :].bitcast(I32))
+        store_codes(nc.scalar, tokens(2, 2))
+        for s in range(SCALE_ROWS):
+            queue = nc.sync if s < SCALE_ROWS // 2 else nc.scalar
+            queue.dma_start(
+                out=out_2[0, s:BLOCKS:SCALE_ROWS, :].bitcast(I32), in_=y_scale[s:P:QUADRANT, :].bitcast(I32)
+            )

from contextlib import ExitStack

import concourse.mybir as mybir
from concourse.masks import make_identity

K, J, T, N = 2048, 512, 512, 512
FLOPS = 2 * (K + J) * T * N

F32 = mybir.dt.float32
BF16 = mybir.dt.bfloat16
I32 = mybir.dt.int32
U32 = mybir.dt.uint32
U16 = mybir.dt.uint16
U8 = mybir.dt.uint8
E4M3X4 = mybir.dt.float8_e4m3fn_x4
E2M1X4 = mybir.dt.float4_e2m1fn_x4

P = 128
PACK = 4
PASSES = K // (P * PACK)
TILES = T // P
BLOCKS = 16
QUADRANT = 32
SCALE_ROWS = 4
LINE = 16
WIDE = P * PACK
BANKS = TILES - 1


def load_scale_rows(nc, plane, rows):
    for s in range(SCALE_ROWS):
        nc.sync.dma_start(
            out=plane[s:P:QUADRANT, :].bitcast(I32).rearrange("q (z c) -> q z c", z=rows.shape[0]),
            in_=rows[:, s:BLOCKS:SCALE_ROWS, :].bitcast(I32).rearrange("z q c -> q z c"),
        )


def tile_list_outlier_channels_pl_kernel(
    tc, xb_words, xb_scales, wb_words, wb_scales, xt, wo_words, wo_scales, offs, out_0, out_1, out_2
):
    nc = tc.nc
    y_rows = out_0.rearrange("(p r) t -> p r t", r=PACK)
    code_rows = out_1[0].rearrange("p c r -> p (c r)").bitcast(I32)

    with ExitStack() as ctx:
        keep = ctx.enter_context(tc.tile_pool(name="keep", bufs=1))
        acc_pool = ctx.enter_context(tc.psum_pool(name="acc", bufs=1))
        turn_pool = ctx.enter_context(tc.psum_pool(name="turn", bufs=2))

        offsets = keep.tile([P, J // 16], U16, name="offsets")
        wb_scale_raw = keep.tile([P, PASSES * N], U8, name="wb_scale_raw", align_bytes=64)
        xb_scale = keep.tile([P, PASSES * T], U8, name="xb_scale", align_bytes=64)
        wo_scale_raw = keep.tile([P, N], U8, name="wo_scale_raw", tag="wo_scale_raw", align_bytes=64)
        ident = keep.tile([P, P], F32, name="ident")
        wb_raw = keep.tile([P, PASSES, N], U32, name="wb_raw")
        xb = keep.tile([P, PASSES, 2 * T], U8, name="xb", align_bytes=64)
        wo_raw = keep.tile([P, 2 * N], U8, name="wo_raw", align_bytes=64)
        rows = [keep.tile([P, K], F32, name="rows%d" % i, tag="rows%d" % i, align_bytes=64) for i in range(TILES)]

        def load_rows(i):
            nc.sync.dma_start(out=rows[i][:], in_=xt[P * i : P * (i + 1), :])

        nc.gpsimd.memset(wb_scale_raw[:].bitcast(U32), 0)
        nc.vector.memset(xb_scale[:].bitcast(U32), 0)
        nc.vector.memset(wo_scale_raw[:].bitcast(U32), 0)
        ident_bf16 = keep.tile([P, P], BF16, name="ident_bf16")
        make_identity(nc, ident_bf16[:])
        nc.scalar.copy(out=ident[:], in_=ident_bf16[:])

        nc.sync.dma_start(out=xb[:].bitcast(I32), in_=xb_words.rearrange("z p c -> p z c").bitcast(I32))
        load_scale_rows(nc, wb_scale_raw, wb_scales)
        nc.sync.dma_start(out=wb_raw[:].bitcast(I32), in_=wb_words.rearrange("z p n r -> p z (n r)").bitcast(I32))
        load_scale_rows(nc, xb_scale, xb_scales)
        load_rows(0)
        nc.sync.dma_start(offsets[:], offs)
        load_rows(1)
        nc.sync.dma_start(out=wo_raw[:].bitcast(I32), in_=wo_words[0].bitcast(I32))
        load_scale_rows(nc, wo_scale_raw, wo_scales)
        load_rows(2)
        load_rows(3)

        wb_scale = [keep.tile([P, N], U8, name="wb_scale%d" % z, align_bytes=64) for z in range(PASSES)]
        wb = [keep.tile([P, N], U32, name="wb%d" % z, align_bytes=64) for z in range(PASSES)]
        wo_scale = keep.tile([P, N], U8, name="wo_scale", align_bytes=64)
        wo = keep.tile([P, N], U16, name="wo", align_bytes=64)

        def deal(dealt, raw, item_bytes):
            run = LINE // item_bytes
            nc.vector.tensor_copy(
                out=dealt.rearrange("p (r c i) -> p c r i", r=PACK, i=run),
                in_=raw.rearrange("p (c i r) -> p c r i", r=PACK, i=run),
            )

        for z in range(PASSES):
            deal(wb_scale[z][:], wb_scale_raw[:, N * z : N * (z + 1)], 1)
        for z in range(PASSES):
            deal(wb[z][:], wb_raw[:, z, :], 4)

        acc = []
        turned = [turn_pool.tile([P, 2, P], F32, name="turned%d" % i, tag="turned") for i in range(TILES)]
        xo = [keep.tile([P, P], U32, name="xo%d" % i, align_bytes=64) for i in range(TILES)]
        xo_scale = [keep.tile([P, P], U8, name="xo_scale%d" % i, align_bytes=64) for i in range(TILES)]
        y = keep.tile([P, PACK, T], F32, name="y")
        y_codes = keep.tile([P, T], U32, name="y_codes", align_bytes=64)
        y_scale = keep.tile([P, T], U8, name="y_scale", align_bytes=64)

        def tokens(first, count):
            return slice(P * first, P * (first + count))

        def base(i):
            acc.append(acc_pool.tile([P, PACK, P], F32, name="acc%d" % i, tag="acc%d" % (i % BANKS)))
            for z in range(PASSES):
                for r in range(PACK):
                    nc.tensor.matmul_mx(
                        out=acc[i][:, r, :],
                        lhsT=wb[z][:, P * r : P * (r + 1)].bitcast(E4M3X4),
                        lhsT_scale=wb_scale[z][:, P * r : P * (r + 1)],
                        rhs=xb[:, z, 2 * P * i : 2 * P * (i + 1)].bitcast(E2M1X4),
                        rhs_scale=xb_scale[:, T * z + P * i : T * z + P * (i + 1)],
                        start=(z == 0 and r == 0),
                        stop=False,
                    )

        def gather(i):
            picked = keep.tile([P, J], BF16, name="picked%d" % i)
            nc.vector.tensor_copy(picked[:], rows[i][:].indirect(offsets[:]))
            pairs = picked[:].bitcast(F32)
            for u in range(2):
                nc.tensor.transpose(turned[i][:, u, :], pairs[:, u : J // 2 : 2], ident[:])

        def quantise_xo(i, staged):
            nc.scalar.copy(
                out=staged.bitcast(F32).rearrange("p (t u) -> p t u", u=2),
                in_=turned[i][:].rearrange("p u t -> p t u"),
            )
            nc.vector.quantize_mx(out=xo[i][:].bitcast(E4M3X4), scales=xo_scale[i][:], in_=staged)

        def finish(i):
            for r in range(PACK):
                nc.tensor.matmul_mx(
                    out=acc[i][:, r, :],
                    lhsT=wo[:, P * r : P * (r + 1)].bitcast(E2M1X4),
                    lhsT_scale=wo_scale[:, P * r : P * (r + 1)],
                    rhs=xo[i][:].bitcast(E4M3X4),
                    rhs_scale=xo_scale[i][:],
                    start=False,
                    stop=(r == PACK - 1),
                )
            nc.scalar.copy(out=y[:, :, tokens(i, 1)], in_=acc[i][:])

        def quantise_y(cols, staged):
            run = LINE // 4
            nc.vector.tensor_copy(
                out=staged.rearrange("p (c i r) -> p c r i", r=PACK, i=run),
                in_=y[:, :, cols].rearrange("p r (c i) -> p c r i", i=run),
            )
            nc.vector.quantize_mx(out=y_codes[:, cols].bitcast(E4M3X4), scales=y_scale[:, cols], in_=staged)

        def store_y(cols):
            nc.sync.dma_start(out=y_rows[:, :, cols], in_=y[:, :, cols])

        def store_codes(queue, cols):
            queue.dma_start(out=code_rows[:, cols], in_=y_codes[:, cols].bitcast(I32))

        def staging(name, tiles, tag):
            return keep.tile([P, tiles * WIDE], BF16, name=name, tag=tag, align_bytes=64)[:]

        gather(0)
        for i in range(BANKS):
            base(i)
        gather(1)
        deal(wo[:], wo_raw[:].bitcast(U16), 2)
        deal(wo_scale[:], wo_scale_raw[:], 1)
        first_in = staging("first_in", 2, "wo_scale_raw")
        quantise_xo(0, first_in[:, 0:WIDE])
        quantise_xo(1, first_in[:, WIDE : 2 * WIDE])
        finish(0)
        finish(1)
        store_y(tokens(0, 2))
        gather(2)
        base(3)
        gather(3)
        after_last = staging("after_last", 3, "rows3")
        quantise_y(tokens(0, 2), after_last[:, 0 : 2 * WIDE])
        store_codes(nc.sync, tokens(0, 2))
        quantise_xo(2, after_last[:, 2 * WIDE : 3 * WIDE])
        finish(2)
        store_y(tokens(2, 1))
        last_in = staging("last_in", 1, "last_in")
        quantise_xo(3, last_in)
        quantise_y(tokens(2, 1), last_in)
        finish(3)
        store_y(tokens(3, 1))
        quantise_y(tokens(3, 1), staging("y_in3", 1, "y_in3"))

        store_codes(nc.scalar, tokens(2, 2))
        for s in range(SCALE_ROWS):
            queue = nc.sync if s < SCALE_ROWS // 2 else nc.scalar
            queue.dma_start(
                out=out_2[0, s:BLOCKS:SCALE_ROWS, :].bitcast(I32), in_=y_scale[s:P:QUADRANT, :].bitcast(I32)
            )
